import numpy as np
import ml_dtypes


def mxq(x, axis, fmt="e4m3"):
    dtype, down = {"e4m3": (ml_dtypes.float8_e4m3fn, 7), "e5m2": (ml_dtypes.float8_e5m2, 14)}[fmt]
    v = np.moveaxis(np.asarray(x, np.float32).astype(ml_dtypes.bfloat16).astype(np.float64), axis, -1)
    blocks = v.reshape(v.shape[:-1] + (-1, 32))
    amax = np.abs(blocks).max(-1, keepdims=True)
    byte = np.maximum(np.where(amax > 0, np.frexp(amax)[1] - 1 + 127, 0) - down, 1)
    scale = np.exp2(byte - 127.0)
    codes = (blocks / scale).astype(np.float32).astype(dtype).astype(np.float64)
    return np.moveaxis((codes * scale).reshape(v.shape), -1, axis)


WIDE = False


def mx_kscale(k):
    if not WIDE:
        return np.ones(k)
    levels = np.array([10, -10, 5, -5, 0])
    if k % 512:
        return np.exp2(np.random.permutation(np.resize(levels, k // 32))).repeat(32)
    a = np.empty((k // 512, 16))
    for p in range(k // 512):
        a[p, :8] = np.random.permutation(np.resize(levels, 8))
        for g in range(8):
            far = levels[np.abs(levels - a[p, g]) >= 10]
            a[p, g + 8] = far[np.random.randint(len(far))]
    return np.exp2(a.ravel()).repeat(32)


def f64(x):
    return np.asarray(x).astype(np.float64)


def striped(idx):
    return np.tile(idx.reshape(-1, 16).T, (8, 1)).astype(np.uint16)


def unstriped(offs):
    return offs[:16].T.reshape(-1).astype(np.int64)


def pack_weight(w):
    k, n = w.shape
    w = f64(np.asarray(w, np.float32).astype(ml_dtypes.bfloat16)).reshape(k // 32, 32, n)
    amax = np.abs(w).max(1)
    byte = np.clip(np.where(amax > 0, np.frexp(amax)[1] - 1 + 127 - 7, 1), 1, 254)
    scaled = (w * np.exp2(127.0 - byte)[:, None, :]).reshape(k, n).astype(np.float32)
    words = np.ascontiguousarray(scaled.reshape(k // 512, 128, 4, n).transpose(0, 1, 3, 2)).astype(ml_dtypes.float8_e4m3fn).view(np.uint8)
    return words, np.ascontiguousarray(byte.astype(np.uint8).reshape(k // 512, 16, n))


def unpack_weight(words, scales):
    g, p, n, _ = words.shape
    vals = np.ascontiguousarray(words).view(ml_dtypes.float8_e4m3fn).astype(np.float64) * np.repeat(np.exp2(scales.astype(np.float64) - 127.0), 8, axis=1)[..., None]
    return vals.transpose(0, 1, 3, 2).reshape(g * 512, n)


K, T, S, N, U = 512, 1024, 512, 128, 512
P = 2 ** 7


def setup_inputs():
    n = np.random.standard_normal
    s = mx_kscale(K)[:, None]
    packed_xT = pack_weight(n((K, T)) * s)
    return {
        "x_words": packed_xT[0],
        "x_scales": packed_xT[1],
        "w1": (n((K, N)) / np.sqrt(K) / s).astype(np.float32),
        "leak": (np.tile(np.random.uniform(0.6, 1.2, U), (P, 1))).astype(np.float32),
        "cur": (np.random.uniform(0.0, 1.5, (N, U))).astype(np.float32),
        "deg": (np.random.uniform(0.2, 0.8, (N, 1))).astype(np.float32),
        "offs": striped(np.random.permutation(T)[:S]),
        "act1": striped(np.random.randint(0, S, U)),
        "act2": striped(np.random.randint(0, S, U)),
        "rep1": striped(np.random.randint(0, S, U)),
    }


def reference(x_words, x_scales, w1, leak, cur, deg, offs, act1, act2, rep1):
    xq = unpack_weight(x_words, x_scales)[:, unstriped(offs)]
    y = mxq(f64(w1), 0, "e4m3").T @ xq
    lev = np.log(np.exp(y) + 1.0)
    ga = lev[:, unstriped(act1)]
    pa = ((ga) ** 2) / ((ga) ** 2 + 0.5)
    gb = lev[:, unstriped(act2)]
    pb = ((gb) ** 2) / ((gb) ** 2 + 0.8)
    gr = lev[:, unstriped(rep1)]
    pr = f64(leak)[:1] / ((gr) ** 2 + 0.7)
    prd = (pa * pb) * pr
    return 1.5 * prd - (f64(deg) * f64(cur))

@@ -1,0 +1,176 @@
+import math
+from contextlib import ExitStack
+
+import concourse.mybir as mybir
+
+K, T, S, N, U = 512, 1024, 512, 128, 512
+FLOPS = 2 * K * N * S
+
+F32 = mybir.dt.float32
+BF16 = mybir.dt.bfloat16
+I32 = mybir.dt.int32
+U32 = mybir.dt.uint32
+U16 = mybir.dt.uint16
+U8 = mybir.dt.uint8
+FP8X4 = mybir.dt.float8_e4m3fn_x4
+ACT = mybir.ActivationFunctionType
+ALU = mybir.AluOpType
+
+P = 128
+PACK = 4
+HALF = 256
+QUARTER = 128
+EXP_CAP = 2.0 ** 60
+LEV_FLOOR = 2.0 ** -60
+
+
+def tile_picked_ygrn_and_p_kernel(
+    tc, x_words, x_scales, w1, leak, cur, deg, offs, act1, act2, rep1, out
+):
+    nc = tc.nc
+    halves = [slice(h * HALF, (h + 1) * HALF) for h in range(2)]
+    quarters = [slice(c * QUARTER, (c + 1) * QUARTER) for c in range(4)]
+
+    with ExitStack() as ctx:
+        sb = ctx.enter_context(tc.tile_pool(name="sb", bufs=1))
+        ps = ctx.enter_context(tc.psum_pool(name="ps", bufs=1))
+
+        offs_t = sb.tile([P, S // 16], U16, name="offs_t")
+        act1_t = sb.tile([P, U // 16], U16, name="act1_t")
+        act2_t = sb.tile([P, U // 16], U16, name="act2_t")
+        rep1_t = sb.tile([P, U // 16], U16, name="rep1_t")
+        words = sb.tile([P, T], U32, name="words", align_bytes=64)
+        scales = sb.tile([P, T], U8, name="scales", tag="scales_then_w_codes", align_bytes=64)
+        w_raw = sb.tile([P, PACK, N], F32, name="w_raw")
+        leak_t = sb.tile([P, U], F32, name="leak_t")
+        cur_t = sb.tile([P, U], F32, name="cur_t")
+        deg_t = sb.tile([P, 1], F32, name="deg_t")
+
+        nc.vector.memset(scales[:].bitcast(I32), 0)
+        nc.scalar.dma_start(out=w_raw[:], in_=w1.rearrange("(p j) n -> p j n", j=PACK))
+        nc.sync.dma_start(out=offs_t[:], in_=offs)
+        for q in range(4):
+            queue = nc.sync if q < 2 else nc.scalar
+            queue.dma_start(
+                out=scales[32 * q : 32 * q + 4, :].bitcast(I32),
+                in_=x_scales[0, 4 * q : 4 * q + 4, :].bitcast(I32),
+            )
+        nc.sync.dma_start(
+            out=words[:].bitcast(I32),
+            in_=x_words[0].rearrange("p n t -> p (n t)").bitcast(I32),
+        )
+        nc.sync.dma_start(out=deg_t[:], in_=deg)
+        nc.sync.dma_start(out=cur_t[:], in_=cur)
+        nc.sync.dma_start(out=act1_t[:], in_=act1)
+        nc.sync.dma_start(out=act2_t[:], in_=act2)
+        nc.sync.dma_start(out=rep1_t[:], in_=rep1)
+        nc.sync.dma_start(out=leak_t[:], in_=leak)
+
+        w_bf = sb.tile([P, N, PACK], BF16, name="w_bf", align_bytes=64)
+        nc.scalar.activation(out=w_bf[:], in_=w_raw[:].rearrange("p j n -> p n j"), func=ACT.Copy)
+
+        picked_scales = sb.tile([P, S], U8, name="picked_scales", align_bytes=64)
+        nc.vector.tensor_copy(out=picked_scales[:], in_=scales[:].indirect(offs_t[:]))
+
+        w_codes = sb.tile([P, N], U32, name="w_codes", tag="scales_then_w_codes", align_bytes=64)
+        w_scales = sb.tile([P, N], U8, name="w_scales", align_bytes=64)
+        nc.vector.quantize_mx(
+            out=w_codes[:].bitcast(FP8X4),
+            scales=w_scales[:],
+            in_=w_bf[:].rearrange("p n j -> p (n j)"),
+        )
+
+        exp_y = sb.tile([P, S], F32, name="exp_y", tag="exp_y_then_decay")
+        y = []
+        for c, cols in enumerate(quarters):
+            picked_words = sb.tile([P, QUARTER], U32, name=f"picked_words{c}", align_bytes=64)
+            nc.vector.tensor_copy(
+                out=picked_words[:], in_=words[:].indirect(offs_t[:, cols.start // 16 : cols.stop // 16])
+            )
+            bank = ps.tile([P, QUARTER], F32, name=f"y{c}")
+            nc.tensor.matmul_mx(
+                out=bank[:],
+                lhsT=w_codes[:].bitcast(FP8X4),
+                lhsT_scale=w_scales[:],
+                rhs=picked_words[:].bitcast(FP8X4),
+                rhs_scale=picked_scales[:, cols],
+                start=True,
+                stop=True,
+            )
+            nc.scalar.activation(out=exp_y[:, cols], in_=bank[:], func=ACT.Exp)
+            y.append(bank)
+
+        exp_p1 = sb.tile([P, S], F32, name="exp_p1")
+        nc.vector.tensor_scalar(
+            out=exp_p1[:], in0=exp_y[:], scalar1=EXP_CAP, scalar2=1.0, op0=ALU.min, op1=ALU.add
+        )
+        decay = sb.tile([P, U], F32, name="decay", tag="exp_y_then_decay")
+        nc.vector.tensor_scalar(
+            out=decay[:], in0=cur_t[:], scalar1=deg_t[:], scalar2=None, op0=ALU.mult
+        )
+
+        capped = sb.tile([P, S], F32, name="capped")
+        lev = sb.tile([P, S], F32, name="lev")
+        log_lev = sb.tile([P, S], F32, name="log_lev")
+        for cols in quarters:
+            nc.scalar.activation(out=capped[:, cols], in_=exp_p1[:, cols], func=ACT.Ln)
+        for c, cols in enumerate(quarters):
+            nc.vector.scalar_tensor_tensor(
+                out=lev[:, cols], in0=y[c][:], scalar=LEV_FLOOR, in1=capped[:, cols],
+                op0=ALU.max, op1=ALU.max,
+            )
+        for cols in quarters:
+            nc.scalar.activation(out=log_lev[:, cols], in_=lev[:, cols], func=ACT.Ln)
+
+        def picked(lst, first, last):
+            return log_lev[:].indirect(lst[:, first // 16 : last // 16])
+
+        def hill(dst, src, sign, const):
+            nc.scalar.activation(
+                out=dst, in_=src, func=ACT.Sigmoid, scale=2.0 * sign, bias=-sign * math.log(const)
+            )
+
+        la = sb.tile([P, U], F32, name="la")
+        lb = sb.tile([P, HALF], F32, name="lb")
+        nc.vector.tensor_copy(out=la[:, :HALF], in_=picked(act1_t, 0, HALF))
+        nc.vector.tensor_copy(out=lb[:], in_=picked(act2_t, 0, HALF))
+        nc.vector.tensor_copy(out=la[:, HALF:], in_=picked(act1_t, HALF, U))
+
+        pa = sb.tile([P, U], F32, name="pa")
+        pb = sb.tile([P, U], F32, name="pb")
+        sr = sb.tile([P, U], F32, name="sr")
+        hill(sr[:, :HALF], picked(rep1_t, 0, HALF), -1.0, 0.7)
+        hill(pa[:, :HALF], la[:, :HALF], 1.0, 0.5)
+        hill(pb[:, :HALF], lb[:], 1.0, 0.8)
+        hill(pa[:, HALF:], la[:, HALF:], 1.0, 0.5)
+        hill(pb[:, HALF:], picked(act2_t, HALF, U), 1.0, 0.8)
+        for cols in quarters[2:]:
+            hill(sr[:, cols], picked(rep1_t, cols.start, cols.stop), -1.0, 0.7)
+
+        t1 = sb.tile([P, U], F32, name="t1")
+        t2 = sb.tile([P, U], F32, name="t2")
+        t3 = sb.tile([P, U], F32, name="t3")
+        res = sb.tile([P, U], F32, name="res")
+
+        def times_leak(src, cols):
+            nc.vector.scalar_tensor_tensor(
+                out=t1[:, cols], in0=src[:, cols], scalar=1.5 / 0.7, in1=leak_t[:, cols], op0=ALU.mult, op1=ALU.mult
+            )
+
+        def mul(dst, a, b, cols):
+            nc.vector.tensor_tensor(out=dst[:, cols], in0=a[:, cols], in1=b[:, cols], op=ALU.mult)
+
+        def finish(cols):
+            nc.vector.tensor_tensor(out=res[:, cols], in0=t3[:, cols], in1=decay[:, cols], op=ALU.subtract)
+            nc.sync.dma_start(out=out[:, cols], in_=res[:, cols])
+
+        times_leak(sr, halves[0])
+        mul(t2, pa, pb, halves[0])
+        times_leak(pa, halves[1])
+        mul(t3, t1, t2, halves[0])
+        mul(t2, t1, pb, halves[1])
+        finish(halves[0])
+        mul(t3, t2, sr, quarters[2])
+        mul(t3, t2, sr, quarters[3])
+        finish(quarters[2])
+        finish(quarters[3])

@@ -50,8 +50,7 @@ def tile_picked_ygrn_and_p_kernel(
         nc.scalar.dma_start(out=w_raw[:], in_=w1.rearrange("(p j) n -> p j n", j=PACK))
         nc.sync.dma_start(out=offs_t[:], in_=offs)
         for q in range(4):
-            queue = nc.sync if q < 2 else nc.scalar
-            queue.dma_start(
+            nc.sync.dma_start(
                 out=scales[32 * q : 32 * q + 4, :].bitcast(I32),
                 in_=x_scales[0, 4 * q : 4 * q + 4, :].bitcast(I32),
             )
@@ -160,17 +159,17 @@ def tile_picked_ygrn_and_p_kernel(
         def mul(dst, a, b, cols):
             nc.vector.tensor_tensor(out=dst[:, cols], in0=a[:, cols], in1=b[:, cols], op=ALU.mult)
 
-        def finish(cols):
+        def finish(cols, queue):
             nc.vector.tensor_tensor(out=res[:, cols], in0=t3[:, cols], in1=decay[:, cols], op=ALU.subtract)
-            nc.sync.dma_start(out=out[:, cols], in_=res[:, cols])
+            queue.dma_start(out=out[:, cols], in_=res[:, cols])
 
         times_leak(sr, halves[0])
         mul(t2, pa, pb, halves[0])
         times_leak(pa, halves[1])
         mul(t3, t1, t2, halves[0])
         mul(t2, t1, pb, halves[1])
-        finish(halves[0])
+        finish(halves[0], nc.sync)
         mul(t3, t2, sr, quarters[2])
         mul(t3, t2, sr, quarters[3])
-        finish(quarters[2])
-        finish(quarters[3])
+        finish(quarters[2], nc.scalar)
+        finish(quarters[3], nc.sync)

import math
from contextlib import ExitStack

import concourse.mybir as mybir

K, T, S, N, U = 512, 1024, 512, 128, 512
FLOPS = 2 * K * N * S

F32 = mybir.dt.float32
BF16 = mybir.dt.bfloat16
I32 = mybir.dt.int32
U32 = mybir.dt.uint32
U16 = mybir.dt.uint16
U8 = mybir.dt.uint8
FP8X4 = mybir.dt.float8_e4m3fn_x4
ACT = mybir.ActivationFunctionType
ALU = mybir.AluOpType

P = 128
PACK = 4
HALF = 256
QUARTER = 128
EXP_CAP = 2.0 ** 60
LEV_FLOOR = 2.0 ** -60


def tile_picked_ygrn_and_p_kernel(
    tc, x_words, x_scales, w1, leak, cur, deg, offs, act1, act2, rep1, out
):
    nc = tc.nc
    halves = [slice(h * HALF, (h + 1) * HALF) for h in range(2)]
    quarters = [slice(c * QUARTER, (c + 1) * QUARTER) for c in range(4)]

    with ExitStack() as ctx:
        sb = ctx.enter_context(tc.tile_pool(name="sb", bufs=1))
        ps = ctx.enter_context(tc.psum_pool(name="ps", bufs=1))

        offs_t = sb.tile([P, S // 16], U16, name="offs_t")
        act1_t = sb.tile([P, U // 16], U16, name="act1_t")
        act2_t = sb.tile([P, U // 16], U16, name="act2_t")
        rep1_t = sb.tile([P, U // 16], U16, name="rep1_t")
        words = sb.tile([P, T], U32, name="words", align_bytes=64)
        scales = sb.tile([P, T], U8, name="scales", tag="scales_then_w_codes", align_bytes=64)
        w_raw = sb.tile([P, PACK, N], F32, name="w_raw")
        leak_t = sb.tile([P, U], F32, name="leak_t")
        cur_t = sb.tile([P, U], F32, name="cur_t")
        deg_t = sb.tile([P, 1], F32, name="deg_t")

        nc.vector.memset(scales[:].bitcast(I32), 0)
        nc.scalar.dma_start(out=w_raw[:], in_=w1.rearrange("(p j) n -> p j n", j=PACK))
        nc.sync.dma_start(out=offs_t[:], in_=offs)
        for q in range(4):
            nc.sync.dma_start(
                out=scales[32 * q : 32 * q + 4, :].bitcast(I32),
                in_=x_scales[0, 4 * q : 4 * q + 4, :].bitcast(I32),
            )
        nc.sync.dma_start(
            out=words[:].bitcast(I32),
            in_=x_words[0].rearrange("p n t -> p (n t)").bitcast(I32),
        )
        nc.sync.dma_start(out=deg_t[:], in_=deg)
        nc.sync.dma_start(out=cur_t[:], in_=cur)
        nc.sync.dma_start(out=act1_t[:], in_=act1)
        nc.sync.dma_start(out=act2_t[:], in_=act2)
        nc.sync.dma_start(out=rep1_t[:], in_=rep1)
        nc.sync.dma_start(out=leak_t[:], in_=leak)

        w_bf = sb.tile([P, N, PACK], BF16, name="w_bf", align_bytes=64)
        nc.scalar.activation(out=w_bf[:], in_=w_raw[:].rearrange("p j n -> p n j"), func=ACT.Copy)

        picked_scales = sb.tile([P, S], U8, name="picked_scales", align_bytes=64)
        nc.vector.tensor_copy(out=picked_scales[:], in_=scales[:].indirect(offs_t[:]))

        w_codes = sb.tile([P, N], U32, name="w_codes", tag="scales_then_w_codes", align_bytes=64)
        w_scales = sb.tile([P, N], U8, name="w_scales", align_bytes=64)
        nc.vector.quantize_mx(
            out=w_codes[:].bitcast(FP8X4),
            scales=w_scales[:],
            in_=w_bf[:].rearrange("p n j -> p (n j)"),
        )

        exp_y = sb.tile([P, S], F32, name="exp_y", tag="exp_y_then_decay")
        y = []
        for c, cols in enumerate(quarters):
            picked_words = sb.tile([P, QUARTER], U32, name=f"picked_words{c}", align_bytes=64)
            nc.vector.tensor_copy(
                out=picked_words[:], in_=words[:].indirect(offs_t[:, cols.start // 16 : cols.stop // 16])
            )
            bank = ps.tile([P, QUARTER], F32, name=f"y{c}")
            nc.tensor.matmul_mx(
                out=bank[:],
                lhsT=w_codes[:].bitcast(FP8X4),
                lhsT_scale=w_scales[:],
                rhs=picked_words[:].bitcast(FP8X4),
                rhs_scale=picked_scales[:, cols],
                start=True,
                stop=True,
            )
            nc.scalar.activation(out=exp_y[:, cols], in_=bank[:], func=ACT.Exp)
            y.append(bank)

        exp_p1 = sb.tile([P, S], F32, name="exp_p1")
        nc.vector.tensor_scalar(
            out=exp_p1[:], in0=exp_y[:], scalar1=EXP_CAP, scalar2=1.0, op0=ALU.min, op1=ALU.add
        )
        decay = sb.tile([P, U], F32, name="decay", tag="exp_y_then_decay")
        nc.vector.tensor_scalar(
            out=decay[:], in0=cur_t[:], scalar1=deg_t[:], scalar2=None, op0=ALU.mult
        )

        capped = sb.tile([P, S], F32, name="capped")
        lev = sb.tile([P, S], F32, name="lev")
        log_lev = sb.tile([P, S], F32, name="log_lev")
        for cols in quarters:
            nc.scalar.activation(out=capped[:, cols], in_=exp_p1[:, cols], func=ACT.Ln)
        for c, cols in enumerate(quarters):
            nc.vector.scalar_tensor_tensor(
                out=lev[:, cols], in0=y[c][:], scalar=LEV_FLOOR, in1=capped[:, cols],
                op0=ALU.max, op1=ALU.max,
            )
        for cols in quarters:
            nc.scalar.activation(out=log_lev[:, cols], in_=lev[:, cols], func=ACT.Ln)

        def picked(lst, first, last):
            return log_lev[:].indirect(lst[:, first // 16 : last // 16])

        def hill(dst, src, sign, const):
            nc.scalar.activation(
                out=dst, in_=src, func=ACT.Sigmoid, scale=2.0 * sign, bias=-sign * math.log(const)
            )

        la = sb.tile([P, U], F32, name="la")
        lb = sb.tile([P, HALF], F32, name="lb")
        nc.vector.tensor_copy(out=la[:, :HALF], in_=picked(act1_t, 0, HALF))
        nc.vector.tensor_copy(out=lb[:], in_=picked(act2_t, 0, HALF))
        nc.vector.tensor_copy(out=la[:, HALF:], in_=picked(act1_t, HALF, U))

        pa = sb.tile([P, U], F32, name="pa")
        pb = sb.tile([P, U], F32, name="pb")
        sr = sb.tile([P, U], F32, name="sr")
        hill(sr[:, :HALF], picked(rep1_t, 0, HALF), -1.0, 0.7)
        hill(pa[:, :HALF], la[:, :HALF], 1.0, 0.5)
        hill(pb[:, :HALF], lb[:], 1.0, 0.8)
        hill(pa[:, HALF:], la[:, HALF:], 1.0, 0.5)
        hill(pb[:, HALF:], picked(act2_t, HALF, U), 1.0, 0.8)
        for cols in quarters[2:]:
            hill(sr[:, cols], picked(rep1_t, cols.start, cols.stop), -1.0, 0.7)

        t1 = sb.tile([P, U], F32, name="t1")
        t2 = sb.tile([P, U], F32, name="t2")
        t3 = sb.tile([P, U], F32, name="t3")
        res = sb.tile([P, U], F32, name="res")

        def times_leak(src, cols):
            nc.vector.scalar_tensor_tensor(
                out=t1[:, cols], in0=src[:, cols], scalar=1.5 / 0.7, in1=leak_t[:, cols], op0=ALU.mult, op1=ALU.mult
            )

        def mul(dst, a, b, cols):
            nc.vector.tensor_tensor(out=dst[:, cols], in0=a[:, cols], in1=b[:, cols], op=ALU.mult)

        def finish(cols, queue):
            nc.vector.tensor_tensor(out=res[:, cols], in0=t3[:, cols], in1=decay[:, cols], op=ALU.subtract)
            queue.dma_start(out=out[:, cols], in_=res[:, cols])

        times_leak(sr, halves[0])
        mul(t2, pa, pb, halves[0])
        times_leak(pa, halves[1])
        mul(t3, t1, t2, halves[0])
        mul(t2, t1, pb, halves[1])
        finish(halves[0], nc.sync)
        mul(t3, t2, sr, quarters[2])
        mul(t3, t2, sr, quarters[3])
        finish(quarters[2], nc.scalar)
        finish(quarters[3], nc.sync)
